import numpy as np
import ml_dtypes


def mxq(x, axis, fmt="e4m3"):
    dtype, down = {"e4m3": (ml_dtypes.float8_e4m3fn, 7), "e5m2": (ml_dtypes.float8_e5m2, 14)}[fmt]
    v = np.moveaxis(np.asarray(x, np.float32).astype(ml_dtypes.bfloat16).astype(np.float64), axis, -1)
    blocks = v.reshape(v.shape[:-1] + (-1, 32))
    amax = np.abs(blocks).max(-1, keepdims=True)
    byte = np.maximum(np.where(amax > 0, np.frexp(amax)[1] - 1 + 127, 0) - down, 1)
    scale = np.exp2(byte - 127.0)
    codes = (blocks / scale).astype(np.float32).astype(dtype).astype(np.float64)
    return np.moveaxis((codes * scale).reshape(v.shape), -1, axis)


WIDE = False


def mx_kscale(k):
    if not WIDE:
        return np.ones(k)
    levels = np.array([10, -10, 5, -5, 0])
    if k % 512:
        return np.exp2(np.random.permutation(np.resize(levels, k // 32))).repeat(32)
    a = np.empty((k // 512, 16))
    for p in range(k // 512):
        a[p, :8] = np.random.permutation(np.resize(levels, 8))
        for g in range(8):
            far = levels[np.abs(levels - a[p, g]) >= 10]
            a[p, g + 8] = far[np.random.randint(len(far))]
    return np.exp2(a.ravel()).repeat(32)


def f64(x):
    return np.asarray(x).astype(np.float64)


def striped(idx):
    return np.tile(idx.reshape(-1, 16).T, (8, 1)).astype(np.uint16)


def unstriped(offs):
    return offs[:16].T.reshape(-1).astype(np.int64)


def pack_weight(w):
    k, n = w.shape
    w = f64(np.asarray(w, np.float32).astype(ml_dtypes.bfloat16)).reshape(k // 32, 32, n)
    amax = np.abs(w).max(1)
    byte = np.clip(np.where(amax > 0, np.frexp(amax)[1] - 1 + 127 - 7, 1), 1, 254)
    scaled = (w * np.exp2(127.0 - byte)[:, None, :]).reshape(k, n).astype(np.float32)
    words = np.ascontiguousarray(scaled.reshape(k // 512, 128, 4, n).transpose(0, 1, 3, 2)).astype(ml_dtypes.float8_e4m3fn).view(np.uint8)
    return words, np.ascontiguousarray(byte.astype(np.uint8).reshape(k // 512, 16, n))


def unpack_weight(words, scales):
    g, p, n, _ = words.shape
    vals = np.ascontiguousarray(words).view(ml_dtypes.float8_e4m3fn).astype(np.float64) * np.repeat(np.exp2(scales.astype(np.float64) - 127.0), 8, axis=1)[..., None]
    return vals.transpose(0, 1, 3, 2).reshape(g * 512, n)


K, T, S, H, N = 512, 4096, 1024, 512, 256


def setup_inputs():
    n = np.random.standard_normal
    s = mx_kscale(K)[:, None]
    u = mx_kscale(H)
    packed_xT = pack_weight(n((K, T)) * s)
    packed_w1 = pack_weight(n((K, N)) / np.sqrt(2 * K) / s)
    packed_w3 = pack_weight(n((H, N)) / np.sqrt(2 * H) / u[:, None])
    return {
        "x_words": packed_xT[0],
        "x_scales": packed_xT[1],
        "w1_words": packed_w1[0],
        "w1_scales": packed_w1[1],
        "w2": (n((K, H)) / np.sqrt(K) / s * u).astype(np.float32),
        "w3_words": packed_w3[0],
        "w3_scales": packed_w3[1],
        "offs": striped(np.random.permutation(T)[:S]),
    }


def reference(x_words, x_scales, w1_words, w1_scales, w2, w3_words, w3_scales, offs):
    xq = unpack_weight(x_words, x_scales)[:, unstriped(offs)]
    h = mxq(f64(w2), 0, "e4m3").T @ xq
    return unpack_weight(w1_words, w1_scales).T @ xq + unpack_weight(w3_words, w3_scales).T @ mxq(h, 0, "e4m3")

@@ -1,0 +1,159 @@
+from contextlib import ExitStack
+
+import concourse.mybir as mybir
+
+K, T, S, H, N = 512, 4096, 1024, 512, 256
+FLOPS = 2 * S * (K * H + K * N + H * N)
+
+F32 = mybir.dt.float32
+BF16 = mybir.dt.bfloat16
+I32 = mybir.dt.int32
+U32 = mybir.dt.uint32
+U16 = mybir.dt.uint16
+U8 = mybir.dt.uint8
+FP8X4 = mybir.dt.float8_e4m3fn_x4
+
+P = 128
+PACK = 4
+HALF = S // 2
+QUARTER = 256
+CHUNK = 128
+LANDING = P - 16
+
+
+def tile_picked_lora_none_p_kernel(
+    tc, x_words, x_scales, w1_words, w1_scales, w2, w3_words, w3_scales, offs, out
+):
+    nc = tc.nc
+    with ExitStack() as ctx:
+        keep = ctx.enter_context(tc.tile_pool(name="keep", bufs=1))
+        psum = ctx.enter_context(tc.psum_pool(name="psum", bufs=4))
+
+        def words_of(dram):
+            return dram[0].rearrange("p n t -> p (n t)").bitcast(I32)
+
+        offsets = keep.tile([P, S // 16], U16, name="offsets")
+        nc.sync.dma_start(offsets[:], offs)
+
+        xs_all = keep.tile([P, T], U8, name="xs_all", align_bytes=64)
+        nc.sync.dma_start(xs_all[LANDING:, :].bitcast(I32), x_scales[0].bitcast(I32))
+        nc.vector.memset(xs_all[:LANDING, :].bitcast(I32), 0)
+
+        w1_codes = keep.tile([P, N], I32, name="w1_codes", align_bytes=64)
+        nc.sync.dma_start(w1_codes[:], words_of(w1_words))
+        xw_all = keep.tile([P, T], I32, name="xw_all", align_bytes=64)
+        nc.sync.dma_start(xw_all[:], words_of(x_words))
+        w2_rows = w2.rearrange("(p j) c -> p j c", j=PACK)
+        w2_raw = []
+        for u in range(2):
+            raw = keep.tile([P, PACK, H // 2], F32, name=f"w2_raw{u}", align_bytes=64)
+            nc.sync.dma_start(raw[:], w2_rows[:, :, u * (H // 2) : (u + 1) * (H // 2)])
+            w2_raw.append(raw)
+        w3_codes = keep.tile([P, N], I32, name="w3_codes", align_bytes=64)
+
+        plane = keep.tile([P, S + 2 * N], U8, name="plane", align_bytes=64)
+        nc.sync.dma_start(w3_codes[:], words_of(w3_words))
+        nc.vector.memset(plane[:LANDING, S:].bitcast(I32), 0)
+        nc.gpsimd.dma_start(plane[LANDING:, S : S + N].bitcast(I32), w1_scales[0].bitcast(I32))
+        nc.gpsimd.dma_start(plane[LANDING:, S + N :].bitcast(I32), w3_scales[0].bitcast(I32))
+        x_plane, w1_plane, w3_plane = plane[:, :S], plane[:, S : S + N], plane[:, S + N :]
+
+        xs_picked = keep.tile([P, S], U8, name="xs_picked", align_bytes=64)
+        nc.vector.tensor_copy(xs_picked[:], xs_all[:].indirect(offsets[:]))
+        nc.vector.tensor_copy(x_plane.bitcast(I32), xs_picked[:].bitcast(I32))
+        for q in range(4):
+            rows = slice(LANDING + 4 * q, LANDING + 4 * q + 4)
+            nc.scalar.dma_start(plane[32 * q : 32 * q + 4, :].bitcast(I32), plane[rows, :].bitcast(I32))
+
+        x_codes = []
+        for u in range(2):
+            picked = keep.tile([P, HALF], U32, name=f"x_codes{u}", align_bytes=64)
+            cols = slice(u * HALF // 16, (u + 1) * HALF // 16)
+            nc.vector.tensor_copy(picked[:], xw_all[:].bitcast(U32).indirect(offsets[:, cols]))
+            x_codes.append(picked)
+
+        def x_operand(start, width):
+            u, c = divmod(start, HALF)
+            return x_codes[u][:, c : c + width].bitcast(FP8X4), x_plane[:, start : start + width]
+
+        def open_out(quarter, tag):
+            banks = []
+            codes, scales = x_operand(quarter * QUARTER, QUARTER)
+            for m in range(N // P):
+                bank = psum.tile([P, QUARTER], F32, name=f"out{quarter}_{m}", tag=tag)
+                cols = slice(m * P, (m + 1) * P)
+                nc.tensor.matmul_mx(
+                    out=bank[:], lhsT=w1_codes[:, cols].bitcast(FP8X4), lhsT_scale=w1_plane[:, cols],
+                    rhs=codes, rhs_scale=scales, start=True, stop=False,
+                )
+                banks.append(bank)
+            return banks
+
+        out_banks = [open_out(0, "early"), open_out(1, "early")]
+
+        M_HALF = P // 2
+        w2_codes = [keep.tile([P, P], U32, name=f"w2_codes{t}", align_bytes=64) for t in range(PACK)]
+        w2_plane = [keep.tile([P, P], U8, name=f"w2_plane{t}", align_bytes=64) for t in range(PACK)]
+        dealt = {}
+        for u, t0, count, copy in (
+            (0, 0, 4, nc.scalar.copy), (1, 0, 2, nc.vector.tensor_copy), (1, 2, 2, nc.scalar.copy)
+        ):
+            tile = keep.tile([P, count, M_HALF, PACK], BF16, name=f"dealt{u}_{t0}", align_bytes=64)
+            src = w2_raw[u][:].rearrange("p j (m t) -> p m t j", t=PACK)[:, :, t0 : t0 + count, :]
+            copy(tile[:].rearrange("p t m j -> p m t j"), src)
+            for t in range(count):
+                dealt[(u, t0 + t)] = tile[:, t].rearrange("p m j -> p (m j)")
+        for u in range(2):
+            for t in range(PACK):
+                cols = slice(u * M_HALF, (u + 1) * M_HALF)
+                nc.vector.quantize_mx(
+                    out=w2_codes[t][:, cols].bitcast(FP8X4), scales=w2_plane[t][:, cols], in_=dealt[(u, t)]
+                )
+
+        h_rounded = [keep.tile([P, QUARTER, PACK], BF16, name=f"h_rounded{q}", align_bytes=64) for q in range(4)]
+        h_codes = [keep.tile([P, QUARTER], U32, name=f"h_codes{q}", align_bytes=64) for q in range(4)]
+        h_plane = [keep.tile([P, QUARTER], U8, name=f"h_plane{q}", align_bytes=64) for q in range(4)]
+
+        def make_h(chunk):
+            bank = psum.tile([P, PACK, CHUNK], F32, name=f"h{chunk}", tag="late")
+            codes, scales = x_operand(chunk * CHUNK, CHUNK)
+            for t in range(PACK):
+                nc.tensor.matmul_mx(
+                    out=bank[:, t, :], lhsT=w2_codes[t][:].bitcast(FP8X4), lhsT_scale=w2_plane[t][:],
+                    rhs=codes, rhs_scale=scales, start=True, stop=True,
+                )
+            q, c = divmod(chunk, 2)
+            copy = nc.vector.tensor_copy if chunk in (1, 3, 5) else nc.scalar.copy
+            copy(h_rounded[q][:, c * CHUNK : (c + 1) * CHUNK, :], bank[:].rearrange("p t n -> p n t"))
+
+        def quantise_h(q):
+            nc.vector.quantize_mx(
+                out=h_codes[q][:].bitcast(FP8X4), scales=h_plane[q][:],
+                in_=h_rounded[q][:].rearrange("p n t -> p (n t)"),
+            )
+
+        def close_out(q):
+            for m, copy in enumerate((nc.scalar.copy, nc.vector.tensor_copy)):
+                cols = slice(m * P, (m + 1) * P)
+                bank = out_banks[q][m]
+                nc.tensor.matmul_mx(
+                    out=bank[:], lhsT=w3_codes[:, cols].bitcast(FP8X4), lhsT_scale=w3_plane[:, cols],
+                    rhs=h_codes[q][:].bitcast(FP8X4), rhs_scale=h_plane[q][:], start=False, stop=True,
+                )
+                result = keep.tile([P, QUARTER], F32, name=f"result{q}_{m}")
+                copy(result[:], bank[:])
+                nc.sync.dma_start(out[cols, q * QUARTER : (q + 1) * QUARTER], result[:])
+
+        for chunk in range(4):
+            make_h(chunk)
+        quantise_h(0)
+        quantise_h(1)
+        for chunk in range(4, 8):
+            make_h(chunk)
+        close_out(0)
+        out_banks.append(open_out(2, "late"))
+        out_banks.append(open_out(3, "late"))
+        quantise_h(2)
+        quantise_h(3)
+        for q in range(1, 4):
+            close_out(q)

@@ -39,23 +39,23 @@ def tile_picked_lora_none_p_kernel(
         nc.sync.dma_start(xs_all[LANDING:, :].bitcast(I32), x_scales[0].bitcast(I32))
         nc.vector.memset(xs_all[:LANDING, :].bitcast(I32), 0)
 
-        w1_codes = keep.tile([P, N], I32, name="w1_codes", align_bytes=64)
-        nc.sync.dma_start(w1_codes[:], words_of(w1_words))
+        plane = keep.tile([P, S + 2 * N], U8, name="plane", align_bytes=64)
+        nc.scalar.dma_start(plane[LANDING:, S : S + N].bitcast(I32), w1_scales[0].bitcast(I32))
+        nc.scalar.dma_start(plane[LANDING:, S + N :].bitcast(I32), w3_scales[0].bitcast(I32))
+        nc.vector.memset(plane[:LANDING, S:].bitcast(I32), 0)
+        seed = keep.tile([P, 2], F32, name="seed")
+        nc.gpsimd.memset(seed[:], 0.0)
+        primed = keep.tile([P, 2], BF16, name="primed")
+        nc.scalar.copy(primed[:], seed[:])
+
+        w2_raw = keep.tile([P, PACK, H], F32, name="w2_raw", align_bytes=64)
+        nc.sync.dma_start(w2_raw[:], w2.rearrange("(p j) c -> p j c", j=PACK))
         xw_all = keep.tile([P, T], I32, name="xw_all", align_bytes=64)
         nc.sync.dma_start(xw_all[:], words_of(x_words))
-        w2_rows = w2.rearrange("(p j) c -> p j c", j=PACK)
-        w2_raw = []
-        for u in range(2):
-            raw = keep.tile([P, PACK, H // 2], F32, name=f"w2_raw{u}", align_bytes=64)
-            nc.sync.dma_start(raw[:], w2_rows[:, :, u * (H // 2) : (u + 1) * (H // 2)])
-            w2_raw.append(raw)
+        w1_codes = keep.tile([P, N], I32, name="w1_codes", align_bytes=64)
+        nc.sync.dma_start(w1_codes[:], words_of(w1_words))
         w3_codes = keep.tile([P, N], I32, name="w3_codes", align_bytes=64)
-
-        plane = keep.tile([P, S + 2 * N], U8, name="plane", align_bytes=64)
         nc.sync.dma_start(w3_codes[:], words_of(w3_words))
-        nc.vector.memset(plane[:LANDING, S:].bitcast(I32), 0)
-        nc.gpsimd.dma_start(plane[LANDING:, S : S + N].bitcast(I32), w1_scales[0].bitcast(I32))
-        nc.gpsimd.dma_start(plane[LANDING:, S + N :].bitcast(I32), w3_scales[0].bitcast(I32))
         x_plane, w1_plane, w3_plane = plane[:, :S], plane[:, S : S + N], plane[:, S + N :]
 
         xs_picked = keep.tile([P, S], U8, name="xs_picked", align_bytes=64)
@@ -65,95 +65,102 @@ def tile_picked_lora_none_p_kernel(
             rows = slice(LANDING + 4 * q, LANDING + 4 * q + 4)
             nc.scalar.dma_start(plane[32 * q : 32 * q + 4, :].bitcast(I32), plane[rows, :].bitcast(I32))
 
-        x_codes = []
+        w2_dealt = keep.tile([P, PACK, P, PACK], BF16, name="w2_dealt", align_bytes=64)
+        for t0, copy in ((0, nc.vector.tensor_copy), (2, nc.scalar.copy)):
+            src = w2_raw[:].rearrange("p j (m t) -> p m t j", t=PACK)[:, :, t0 : t0 + 2, :]
+            copy(w2_dealt[:, t0 : t0 + 2].rearrange("p t m j -> p m t j"), src)
+        w2_codes = keep.tile([P, H], U32, name="w2_codes", align_bytes=64)
+        w2_plane = keep.tile([P, H], U8, name="w2_plane", align_bytes=64)
+        nc.vector.quantize_mx(
+            out=w2_codes[:].bitcast(FP8X4), scales=w2_plane[:], in_=w2_dealt[:].rearrange("p t m j -> p (t m j)")
+        )
+        warm = psum.tile([P, H], F32, name="warm", tag="late")
+        for turn in range(4):
+            nc.tensor.matmul_mx(
+                out=warm[:], lhsT=w2_codes[:, :P].bitcast(FP8X4), lhsT_scale=w2_plane[:, :P],
+                rhs=w2_codes[:].bitcast(FP8X4), rhs_scale=w2_plane[:], start=True, stop=True,
+            )
+
+        x_codes = keep.tile([P, S], U32, name="x_codes", align_bytes=64)
         for u in range(2):
-            picked = keep.tile([P, HALF], U32, name=f"x_codes{u}", align_bytes=64)
-            cols = slice(u * HALF // 16, (u + 1) * HALF // 16)
-            nc.vector.tensor_copy(picked[:], xw_all[:].bitcast(U32).indirect(offsets[:, cols]))
-            x_codes.append(picked)
+            nc.vector.tensor_copy(
+                x_codes[:, u * HALF : (u + 1) * HALF],
+                xw_all[:].bitcast(U32).indirect(offsets[:, u * HALF // 16 : (u + 1) * HALF // 16]),
+            )
 
-        def x_operand(start, width):
-            u, c = divmod(start, HALF)
-            return x_codes[u][:, c : c + width].bitcast(FP8X4), x_plane[:, start : start + width]
-
-        def open_out(quarter, tag):
-            banks = []
-            codes, scales = x_operand(quarter * QUARTER, QUARTER)
-            for m in range(N // P):
-                bank = psum.tile([P, QUARTER], F32, name=f"out{quarter}_{m}", tag=tag)
-                cols = slice(m * P, (m + 1) * P)
-                nc.tensor.matmul_mx(
-                    out=bank[:], lhsT=w1_codes[:, cols].bitcast(FP8X4), lhsT_scale=w1_plane[:, cols],
-                    rhs=codes, rhs_scale=scales, start=True, stop=False,
-                )
-                banks.append(bank)
-            return banks
-
-        out_banks = [open_out(0, "early"), open_out(1, "early")]
-
-        M_HALF = P // 2
-        w2_codes = [keep.tile([P, P], U32, name=f"w2_codes{t}", align_bytes=64) for t in range(PACK)]
-        w2_plane = [keep.tile([P, P], U8, name=f"w2_plane{t}", align_bytes=64) for t in range(PACK)]
-        dealt = {}
-        for u, t0, count, copy in (
-            (0, 0, 4, nc.scalar.copy), (1, 0, 2, nc.vector.tensor_copy), (1, 2, 2, nc.scalar.copy)
-        ):
-            tile = keep.tile([P, count, M_HALF, PACK], BF16, name=f"dealt{u}_{t0}", align_bytes=64)
-            src = w2_raw[u][:].rearrange("p j (m t) -> p m t j", t=PACK)[:, :, t0 : t0 + count, :]
-            copy(tile[:].rearrange("p t m j -> p m t j"), src)
-            for t in range(count):
-                dealt[(u, t0 + t)] = tile[:, t].rearrange("p m j -> p (m j)")
-        for u in range(2):
-            for t in range(PACK):
-                cols = slice(u * M_HALF, (u + 1) * M_HALF)
-                nc.vector.quantize_mx(
-                    out=w2_codes[t][:, cols].bitcast(FP8X4), scales=w2_plane[t][:, cols], in_=dealt[(u, t)]
-                )
-
-        h_rounded = [keep.tile([P, QUARTER, PACK], BF16, name=f"h_rounded{q}", align_bytes=64) for q in range(4)]
-        h_codes = [keep.tile([P, QUARTER], U32, name=f"h_codes{q}", align_bytes=64) for q in range(4)]
-        h_plane = [keep.tile([P, QUARTER], U8, name=f"h_plane{q}", align_bytes=64) for q in range(4)]
+        edges = (0, 1, 3, 5, 7, 8)
+        groups = [slice(a * CHUNK, b * CHUNK) for a, b in zip(edges, edges[1:])]
+        h_rounded = keep.tile([P, S * PACK], BF16, name="h_rounded", align_bytes=64)
+        h_codes = keep.tile([P, S], U32, name="h_codes", align_bytes=64)
+        h_plane = keep.tile([P, S], U8, name="h_plane", align_bytes=64)
+        out_banks = {}
 
         def make_h(chunk):
             bank = psum.tile([P, PACK, CHUNK], F32, name=f"h{chunk}", tag="late")
-            codes, scales = x_operand(chunk * CHUNK, CHUNK)
+            tokens = slice(chunk * CHUNK, (chunk + 1) * CHUNK)
             for t in range(PACK):
+                cols = slice(t * P, (t + 1) * P)
                 nc.tensor.matmul_mx(
-                    out=bank[:, t, :], lhsT=w2_codes[t][:].bitcast(FP8X4), lhsT_scale=w2_plane[t][:],
-                    rhs=codes, rhs_scale=scales, start=True, stop=True,
+                    out=bank[:, t, :], lhsT=w2_codes[:, cols].bitcast(FP8X4), lhsT_scale=w2_plane[:, cols],
+                    rhs=x_codes[:, tokens].bitcast(FP8X4), rhs_scale=x_plane[:, tokens], start=True, stop=True,
                 )
-            q, c = divmod(chunk, 2)
             copy = nc.vector.tensor_copy if chunk in (1, 3, 5) else nc.scalar.copy
-            copy(h_rounded[q][:, c * CHUNK : (c + 1) * CHUNK, :], bank[:].rearrange("p t n -> p n t"))
+            dst = h_rounded[:, tokens.start * PACK : tokens.stop * PACK].rearrange("p (n t) -> p n t", t=PACK)
+            copy(dst, bank[:].rearrange("p t n -> p n t"))
 
-        def quantise_h(q):
+        def quantise_h(g):
+            tokens = groups[g]
             nc.vector.quantize_mx(
-                out=h_codes[q][:].bitcast(FP8X4), scales=h_plane[q][:],
-                in_=h_rounded[q][:].rearrange("p n t -> p (n t)"),
+                out=h_codes[:, tokens].bitcast(FP8X4), scales=h_plane[:, tokens],
+                in_=h_rounded[:, tokens.start * PACK : tokens.stop * PACK],
             )
 
-        def close_out(q):
-            for m, copy in enumerate((nc.scalar.copy, nc.vector.tensor_copy)):
+        def open_out(g, tag):
+            tokens = groups[g]
+            for m in range(N // P):
+                bank = psum.tile([P, tokens.stop - tokens.start], F32, name=f"out{g}_{m}", tag=tag)
                 cols = slice(m * P, (m + 1) * P)
-                bank = out_banks[q][m]
+                nc.tensor.matmul_mx(
+                    out=bank[:], lhsT=w1_codes[:, cols].bitcast(FP8X4), lhsT_scale=w1_plane[:, cols],
+                    rhs=x_codes[:, tokens].bitcast(FP8X4), rhs_scale=x_plane[:, tokens], start=True, stop=False,
+                )
+                out_banks[(g, m)] = bank
+
+        def close_out(g):
+            tokens = groups[g]
+            for m in range(N // P):
+                cols = slice(m * P, (m + 1) * P)
+                bank = out_banks[(g, m)]
                 nc.tensor.matmul_mx(
                     out=bank[:], lhsT=w3_codes[:, cols].bitcast(FP8X4), lhsT_scale=w3_plane[:, cols],
-                    rhs=h_codes[q][:].bitcast(FP8X4), rhs_scale=h_plane[q][:], start=False, stop=True,
+                    rhs=h_codes[:, tokens].bitcast(FP8X4), rhs_scale=h_plane[:, tokens], start=False, stop=True,
                 )
-                result = keep.tile([P, QUARTER], F32, name=f"result{q}_{m}")
+                result = keep.tile([P, tokens.stop - tokens.start], F32, name=f"result{g}_{m}")
+                copy = nc.vector.tensor_copy if m == 0 and g > 0 else nc.scalar.copy
                 copy(result[:], bank[:])
-                nc.sync.dma_start(out[cols, q * QUARTER : (q + 1) * QUARTER], result[:])
+                queue = nc.scalar if (g, m) == (len(groups) - 1, 1) else nc.sync
+                queue.dma_start(out[cols, tokens], result[:])
 
-        for chunk in range(4):
-            make_h(chunk)
+        make_h(0)
+        make_h(1)
+        open_out(0, "early")
         quantise_h(0)
+        make_h(2)
+        open_out(1, "early")
+        make_h(3)
         quantise_h(1)
-        for chunk in range(4, 8):
-            make_h(chunk)
+        make_h(4)
         close_out(0)
-        out_banks.append(open_out(2, "late"))
-        out_banks.append(open_out(3, "late"))
+        make_h(5)
         quantise_h(2)
+        open_out(2, "early")
+        make_h(6)
+        close_out(1)
+        make_h(7)
         quantise_h(3)
-        for q in range(1, 4):
-            close_out(q)
+        open_out(3, "late")
+        close_out(2)
+        quantise_h(4)
+        open_out(4, "late")
+        close_out(3)
+        close_out(4)

@@ -15,10 +15,12 @@ FP8X4 = mybir.dt.float8_e4m3fn_x4
 
 P = 128
 PACK = 4
+PER_COLUMN = 16
+SCALE_ROWS = 16
+LANDING = P - SCALE_ROWS
 HALF = S // 2
-QUARTER = 256
 CHUNK = 128
-LANDING = P - 16
+WARM_PASSES = 4
 
 
 def tile_picked_lora_none_p_kernel(
@@ -32,7 +34,7 @@ def tile_picked_lora_none_p_kernel(
         def words_of(dram):
             return dram[0].rearrange("p n t -> p (n t)").bitcast(I32)
 
-        offsets = keep.tile([P, S // 16], U16, name="offsets")
+        offsets = keep.tile([P, S // PER_COLUMN], U16, name="offsets")
         nc.sync.dma_start(offsets[:], offs)
 
         xs_all = keep.tile([P, T], U8, name="xs_all", align_bytes=64)
@@ -43,6 +45,7 @@ def tile_picked_lora_none_p_kernel(
         nc.scalar.dma_start(plane[LANDING:, S : S + N].bitcast(I32), w1_scales[0].bitcast(I32))
         nc.scalar.dma_start(plane[LANDING:, S + N :].bitcast(I32), w3_scales[0].bitcast(I32))
         nc.vector.memset(plane[:LANDING, S:].bitcast(I32), 0)
+
         seed = keep.tile([P, 2], F32, name="seed")
         nc.gpsimd.memset(seed[:], 0.0)
         primed = keep.tile([P, 2], BF16, name="primed")
@@ -66,16 +69,17 @@ def tile_picked_lora_none_p_kernel(
             nc.scalar.dma_start(plane[32 * q : 32 * q + 4, :].bitcast(I32), plane[rows, :].bitcast(I32))
 
         w2_dealt = keep.tile([P, PACK, P, PACK], BF16, name="w2_dealt", align_bytes=64)
-        for t0, copy in ((0, nc.vector.tensor_copy), (2, nc.scalar.copy)):
-            src = w2_raw[:].rearrange("p j (m t) -> p m t j", t=PACK)[:, :, t0 : t0 + 2, :]
-            copy(w2_dealt[:, t0 : t0 + 2].rearrange("p t m j -> p m t j"), src)
+        nc.vector.tensor_copy(
+            w2_dealt[:].rearrange("p t m j -> p m t j"), w2_raw[:].rearrange("p j (m t) -> p m t j", t=PACK)
+        )
         w2_codes = keep.tile([P, H], U32, name="w2_codes", align_bytes=64)
         w2_plane = keep.tile([P, H], U8, name="w2_plane", align_bytes=64)
         nc.vector.quantize_mx(
             out=w2_codes[:].bitcast(FP8X4), scales=w2_plane[:], in_=w2_dealt[:].rearrange("p t m j -> p (t m j)")
         )
+
         warm = psum.tile([P, H], F32, name="warm", tag="late")
-        for turn in range(4):
+        for turn in range(WARM_PASSES):
             nc.tensor.matmul_mx(
                 out=warm[:], lhsT=w2_codes[:, :P].bitcast(FP8X4), lhsT_scale=w2_plane[:, :P],
                 rhs=w2_codes[:].bitcast(FP8X4), rhs_scale=w2_plane[:], start=True, stop=True,
@@ -94,6 +98,7 @@ def tile_picked_lora_none_p_kernel(
         h_codes = keep.tile([P, S], U32, name="h_codes", align_bytes=64)
         h_plane = keep.tile([P, S], U8, name="h_plane", align_bytes=64)
         out_banks = {}
+        chunks = S // CHUNK
 
         def make_h(chunk):
             bank = psum.tile([P, PACK, CHUNK], F32, name=f"h{chunk}", tag="late")
@@ -142,25 +147,13 @@ def tile_picked_lora_none_p_kernel(
                 queue.dma_start(out[cols, tokens], result[:])
 
         make_h(0)
-        make_h(1)
-        open_out(0, "early")
-        quantise_h(0)
-        make_h(2)
-        open_out(1, "early")
-        make_h(3)
-        quantise_h(1)
-        make_h(4)
-        close_out(0)
-        make_h(5)
-        quantise_h(2)
-        open_out(2, "early")
-        make_h(6)
-        close_out(1)
-        make_h(7)
-        quantise_h(3)
-        open_out(3, "late")
-        close_out(2)
-        quantise_h(4)
-        open_out(4, "late")
-        close_out(3)
-        close_out(4)
+        for g in range(len(groups)):
+            if 2 * g + 1 < chunks:
+                make_h(2 * g + 1)
+            quantise_h(g)
+            open_out(g, "early" if g < 3 else "late")
+            if 2 * g + 2 < chunks:
+                make_h(2 * g + 2)
+            if g > 0:
+                close_out(g - 1)
+        close_out(len(groups) - 1)

@@ -29,7 +29,7 @@ def tile_picked_lora_none_p_kernel(
     nc = tc.nc
     with ExitStack() as ctx:
         keep = ctx.enter_context(tc.tile_pool(name="keep", bufs=1))
-        psum = ctx.enter_context(tc.psum_pool(name="psum", bufs=4))
+        psum = ctx.enter_context(tc.psum_pool(name="psum", bufs=8))
 
         def words_of(dram):
             return dram[0].rearrange("p n t -> p (n t)").bitcast(I32)
@@ -78,7 +78,7 @@ def tile_picked_lora_none_p_kernel(
             out=w2_codes[:].bitcast(FP8X4), scales=w2_plane[:], in_=w2_dealt[:].rearrange("p t m j -> p (t m j)")
         )
 
-        warm = psum.tile([P, H], F32, name="warm", tag="late")
+        warm = psum.tile([P, H], F32, name="warm", tag="bank")
         for turn in range(WARM_PASSES):
             nc.tensor.matmul_mx(
                 out=warm[:], lhsT=w2_codes[:, :P].bitcast(FP8X4), lhsT_scale=w2_plane[:, :P],
@@ -98,10 +98,9 @@ def tile_picked_lora_none_p_kernel(
         h_codes = keep.tile([P, S], U32, name="h_codes", align_bytes=64)
         h_plane = keep.tile([P, S], U8, name="h_plane", align_bytes=64)
         out_banks = {}
-        chunks = S // CHUNK
 
         def make_h(chunk):
-            bank = psum.tile([P, PACK, CHUNK], F32, name=f"h{chunk}", tag="late")
+            bank = psum.tile([P, PACK, CHUNK], F32, name=f"h{chunk}", tag="bank")
             tokens = slice(chunk * CHUNK, (chunk + 1) * CHUNK)
             for t in range(PACK):
                 cols = slice(t * P, (t + 1) * P)
@@ -109,7 +108,7 @@ def tile_picked_lora_none_p_kernel(
                     out=bank[:, t, :], lhsT=w2_codes[:, cols].bitcast(FP8X4), lhsT_scale=w2_plane[:, cols],
                     rhs=x_codes[:, tokens].bitcast(FP8X4), rhs_scale=x_plane[:, tokens], start=True, stop=True,
                 )
-            copy = nc.vector.tensor_copy if chunk in (1, 3, 5) else nc.scalar.copy
+            copy = nc.vector.tensor_copy if chunk in (1, 3) else nc.scalar.copy
             dst = h_rounded[:, tokens.start * PACK : tokens.stop * PACK].rearrange("p (n t) -> p n t", t=PACK)
             copy(dst, bank[:].rearrange("p t n -> p n t"))
 
@@ -120,40 +119,72 @@ def tile_picked_lora_none_p_kernel(
                 in_=h_rounded[:, tokens.start * PACK : tokens.stop * PACK],
             )
 
-        def open_out(g, tag):
+        def pass_out(bank, codes, scales, m, moving, moving_scales, tokens, first):
+            cols = slice(m * P, (m + 1) * P)
+            nc.tensor.matmul_mx(
+                out=bank, lhsT=codes[:, cols].bitcast(FP8X4), lhsT_scale=scales[:, cols],
+                rhs=moving[:, tokens].bitcast(FP8X4), rhs_scale=moving_scales[:, tokens], start=first, stop=not first,
+            )
+
+        def open_out(g):
             tokens = groups[g]
             for m in range(N // P):
-                bank = psum.tile([P, tokens.stop - tokens.start], F32, name=f"out{g}_{m}", tag=tag)
-                cols = slice(m * P, (m + 1) * P)
-                nc.tensor.matmul_mx(
-                    out=bank[:], lhsT=w1_codes[:, cols].bitcast(FP8X4), lhsT_scale=w1_plane[:, cols],
-                    rhs=x_codes[:, tokens].bitcast(FP8X4), rhs_scale=x_plane[:, tokens], start=True, stop=False,
-                )
+                bank = psum.tile([P, tokens.stop - tokens.start], F32, name=f"out{g}_{m}", tag="bank")
+                pass_out(bank[:], w1_codes, w1_plane, m, x_codes, x_plane, tokens, True)
                 out_banks[(g, m)] = bank
 
         def close_out(g):
-            tokens = groups[g]
             for m in range(N // P):
-                cols = slice(m * P, (m + 1) * P)
-                bank = out_banks[(g, m)]
-                nc.tensor.matmul_mx(
-                    out=bank[:], lhsT=w3_codes[:, cols].bitcast(FP8X4), lhsT_scale=w3_plane[:, cols],
-                    rhs=h_codes[:, tokens].bitcast(FP8X4), rhs_scale=h_plane[:, tokens], start=False, stop=True,
-                )
-                result = keep.tile([P, tokens.stop - tokens.start], F32, name=f"result{g}_{m}")
-                copy = nc.vector.tensor_copy if m == 0 and g > 0 else nc.scalar.copy
-                copy(result[:], bank[:])
-                queue = nc.scalar if (g, m) == (len(groups) - 1, 1) else nc.sync
-                queue.dma_start(out[cols, tokens], result[:])
+                pass_out(out_banks[(g, m)][:], w3_codes, w3_plane, m, h_codes, h_plane, groups[g], False)
 
+        def store_out(g, m, copy, queue):
+            tokens = groups[g]
+            result = keep.tile([P, tokens.stop - tokens.start], F32, name=f"result{g}_{m}")
+            copy(result[:], out_banks[(g, m)][:])
+            queue.dma_start(out[m * P : (m + 1) * P, tokens], result[:])
+
+        def first_out():
+            tokens = groups[0]
+            bank = psum.tile([P, N // P, CHUNK], F32, name="out0", tag="bank")
+            for m in range(N // P):
+                pass_out(bank[:, m, :], w1_codes, w1_plane, m, x_codes, x_plane, tokens, True)
+                pass_out(bank[:, m, :], w3_codes, w3_plane, m, h_codes, h_plane, tokens, False)
+            return bank
+
+        def first_store(bank):
+            result = keep.tile([P, N // P, CHUNK], F32, name="result0")
+            nc.vector.tensor_copy(result[:], bank[:])
+            nc.sync.dma_start(out.rearrange("(m p) s -> p m s", p=P)[:, :, groups[0]], result[:])
+
+        vector, scalar = nc.vector.tensor_copy, nc.scalar.copy
         make_h(0)
-        for g in range(len(groups)):
-            if 2 * g + 1 < chunks:
-                make_h(2 * g + 1)
-            quantise_h(g)
-            open_out(g, "early" if g < 3 else "late")
-            if 2 * g + 2 < chunks:
-                make_h(2 * g + 2)
-            if g > 0:
-                close_out(g - 1)
-        close_out(len(groups) - 1)
+        make_h(1)
+        make_h(2)
+        quantise_h(0)
+        make_h(3)
+        make_h(4)
+        make_h(5)
+        quantise_h(1)
+        bank0 = first_out()
+        make_h(6)
+        quantise_h(2)
+        first_store(bank0)
+        open_out(1)
+        close_out(1)
+        make_h(7)
+        store_out(1, 0, vector, nc.sync)
+        store_out(1, 1, vector, nc.sync)
+        open_out(2)
+        close_out(2)
+        quantise_h(3)
+        store_out(2, 0, vector, nc.sync)
+        store_out(2, 1, scalar, nc.sync)
+        open_out(3)
+        open_out(4)
+        quantise_h(4)
+        close_out(3)
+        store_out(3, 0, vector, nc.sync)
+        store_out(3, 1, scalar, nc.sync)
+        close_out(4)
+        store_out(4, 0, vector, nc.sync)
+        store_out(4, 1, scalar, nc.scalar)

@@ -154,7 +154,8 @@ def tile_picked_lora_none_p_kernel(
         def first_store(bank):
             result = keep.tile([P, N // P, CHUNK], F32, name="result0")
             nc.vector.tensor_copy(result[:], bank[:])
-            nc.sync.dma_start(out.rearrange("(m p) s -> p m s", p=P)[:, :, groups[0]], result[:])
+            for m in range(N // P):
+                nc.sync.dma_start(out[m * P : (m + 1) * P, groups[0]], result[:, m, :])
 
         vector, scalar = nc.vector.tensor_copy, nc.scalar.copy
         make_h(0)

@@ -14,12 +14,19 @@ U8 = mybir.dt.uint8
 FP8X4 = mybir.dt.float8_e4m3fn_x4
 
 P = 128
+BANKS = 8
+QUADRANT = 32
 PACK = 4
 PER_COLUMN = 16
 SCALE_ROWS = 16
 LANDING = P - SCALE_ROWS
 HALF = S // 2
 CHUNK = 128
+CHUNKS = S // CHUNK
+GROUP_EDGES = (0, 1, 3, 5, 7, 8)
+VECTOR_CHUNKS = (1, 3)
+LEAD = BANKS - N // P
+VECTOR_GROUPS = 2
 WARM_PASSES = 4
 
 
@@ -29,7 +36,7 @@ def tile_picked_lora_none_p_kernel(
     nc = tc.nc
     with ExitStack() as ctx:
         keep = ctx.enter_context(tc.tile_pool(name="keep", bufs=1))
-        psum = ctx.enter_context(tc.psum_pool(name="psum", bufs=8))
+        psum = ctx.enter_context(tc.psum_pool(name="psum", bufs=BANKS))
 
         def words_of(dram):
             return dram[0].rearrange("p n t -> p (n t)").bitcast(I32)
@@ -41,10 +48,11 @@ def tile_picked_lora_none_p_kernel(
         nc.sync.dma_start(xs_all[LANDING:, :].bitcast(I32), x_scales[0].bitcast(I32))
         nc.vector.memset(xs_all[:LANDING, :].bitcast(I32), 0)
 
-        plane = keep.tile([P, S + 2 * N], U8, name="plane", align_bytes=64)
-        nc.scalar.dma_start(plane[LANDING:, S : S + N].bitcast(I32), w1_scales[0].bitcast(I32))
-        nc.scalar.dma_start(plane[LANDING:, S + N :].bitcast(I32), w3_scales[0].bitcast(I32))
-        nc.vector.memset(plane[:LANDING, S:].bitcast(I32), 0)
+        planes = keep.tile([P, S + 2 * N], U8, name="planes", align_bytes=64)
+        nc.scalar.dma_start(planes[LANDING:, S : S + N].bitcast(I32), w1_scales[0].bitcast(I32))
+        nc.scalar.dma_start(planes[LANDING:, S + N :].bitcast(I32), w3_scales[0].bitcast(I32))
+        nc.vector.memset(planes[:LANDING, S:].bitcast(I32), 0)
+        x_plane, w1_plane, w3_plane = planes[:, :S], planes[:, S : S + N], planes[:, S + N :]
 
         seed = keep.tile([P, 2], F32, name="seed")
         nc.gpsimd.memset(seed[:], 0.0)
@@ -59,14 +67,16 @@ def tile_picked_lora_none_p_kernel(
         nc.sync.dma_start(w1_codes[:], words_of(w1_words))
         w3_codes = keep.tile([P, N], I32, name="w3_codes", align_bytes=64)
         nc.sync.dma_start(w3_codes[:], words_of(w3_words))
-        x_plane, w1_plane, w3_plane = plane[:, :S], plane[:, S : S + N], plane[:, S + N :]
 
         xs_picked = keep.tile([P, S], U8, name="xs_picked", align_bytes=64)
         nc.vector.tensor_copy(xs_picked[:], xs_all[:].indirect(offsets[:]))
         nc.vector.tensor_copy(x_plane.bitcast(I32), xs_picked[:].bitcast(I32))
-        for q in range(4):
-            rows = slice(LANDING + 4 * q, LANDING + 4 * q + 4)
-            nc.scalar.dma_start(plane[32 * q : 32 * q + 4, :].bitcast(I32), plane[rows, :].bitcast(I32))
+        rows = SCALE_ROWS * QUADRANT // P
+        for q in range(P // QUADRANT):
+            nc.scalar.dma_start(
+                planes[QUADRANT * q : QUADRANT * q + rows, :].bitcast(I32),
+                planes[LANDING + rows * q : LANDING + rows * (q + 1), :].bitcast(I32),
+            )
 
         w2_dealt = keep.tile([P, PACK, P, PACK], BF16, name="w2_dealt", align_bytes=64)
         nc.vector.tensor_copy(
@@ -86,18 +96,16 @@ def tile_picked_lora_none_p_kernel(
             )
 
         x_codes = keep.tile([P, S], U32, name="x_codes", align_bytes=64)
-        for u in range(2):
+        for first in range(0, S, HALF):
             nc.vector.tensor_copy(
-                x_codes[:, u * HALF : (u + 1) * HALF],
-                xw_all[:].bitcast(U32).indirect(offsets[:, u * HALF // 16 : (u + 1) * HALF // 16]),
+                x_codes[:, first : first + HALF],
+                xw_all[:].bitcast(U32).indirect(offsets[:, first // PER_COLUMN : (first + HALF) // PER_COLUMN]),
             )
 
-        edges = (0, 1, 3, 5, 7, 8)
-        groups = [slice(a * CHUNK, b * CHUNK) for a, b in zip(edges, edges[1:])]
+        groups = [slice(a * CHUNK, b * CHUNK) for a, b in zip(GROUP_EDGES, GROUP_EDGES[1:])]
         h_rounded = keep.tile([P, S * PACK], BF16, name="h_rounded", align_bytes=64)
         h_codes = keep.tile([P, S], U32, name="h_codes", align_bytes=64)
         h_plane = keep.tile([P, S], U8, name="h_plane", align_bytes=64)
-        out_banks = {}
 
         def make_h(chunk):
             bank = psum.tile([P, PACK, CHUNK], F32, name=f"h{chunk}", tag="bank")
@@ -108,9 +116,9 @@ def tile_picked_lora_none_p_kernel(
                     out=bank[:, t, :], lhsT=w2_codes[:, cols].bitcast(FP8X4), lhsT_scale=w2_plane[:, cols],
                     rhs=x_codes[:, tokens].bitcast(FP8X4), rhs_scale=x_plane[:, tokens], start=True, stop=True,
                 )
-            copy = nc.vector.tensor_copy if chunk in (1, 3) else nc.scalar.copy
-            dst = h_rounded[:, tokens.start * PACK : tokens.stop * PACK].rearrange("p (n t) -> p n t", t=PACK)
-            copy(dst, bank[:].rearrange("p t n -> p n t"))
+            copy = nc.vector.tensor_copy if chunk in VECTOR_CHUNKS else nc.scalar.copy
+            interleaved = h_rounded[:, tokens.start * PACK : tokens.stop * PACK].rearrange("p (n t) -> p n t", t=PACK)
+            copy(interleaved, bank[:].rearrange("p t n -> p n t"))
 
         def quantise_h(g):
             tokens = groups[g]
@@ -119,73 +127,39 @@ def tile_picked_lora_none_p_kernel(
                 in_=h_rounded[:, tokens.start * PACK : tokens.stop * PACK],
             )
 
-        def pass_out(bank, codes, scales, m, moving, moving_scales, tokens, first):
-            cols = slice(m * P, (m + 1) * P)
-            nc.tensor.matmul_mx(
-                out=bank, lhsT=codes[:, cols].bitcast(FP8X4), lhsT_scale=scales[:, cols],
-                rhs=moving[:, tokens].bitcast(FP8X4), rhs_scale=moving_scales[:, tokens], start=first, stop=not first,
-            )
-
-        def open_out(g):
+        def multiply_out(g):
             tokens = groups[g]
-            for m in range(N // P):
-                bank = psum.tile([P, tokens.stop - tokens.start], F32, name=f"out{g}_{m}", tag="bank")
-                pass_out(bank[:], w1_codes, w1_plane, m, x_codes, x_plane, tokens, True)
-                out_banks[(g, m)] = bank
+            width = tokens.stop - tokens.start
+            banks = [psum.tile([P, width], F32, name=f"out{g}_{m}", tag="bank") for m in range(N // P)]
+            terms = ((w1_codes, w1_plane, x_codes, x_plane), (w3_codes, w3_plane, h_codes, h_plane))
+            for term, (w_codes, w_plane, codes, plane) in enumerate(terms):
+                for m, bank in enumerate(banks):
+                    cols = slice(m * P, (m + 1) * P)
+                    nc.tensor.matmul_mx(
+                        out=bank[:], lhsT=w_codes[:, cols].bitcast(FP8X4), lhsT_scale=w_plane[:, cols],
+                        rhs=codes[:, tokens].bitcast(FP8X4), rhs_scale=plane[:, tokens],
+                        start=term == 0, stop=term == len(terms) - 1,
+                    )
+            return banks
 
-        def close_out(g):
-            for m in range(N // P):
-                pass_out(out_banks[(g, m)][:], w3_codes, w3_plane, m, h_codes, h_plane, groups[g], False)
-
-        def store_out(g, m, copy, queue):
+        def store_out(g, banks):
             tokens = groups[g]
-            result = keep.tile([P, tokens.stop - tokens.start], F32, name=f"result{g}_{m}")
-            copy(result[:], out_banks[(g, m)][:])
-            queue.dma_start(out[m * P : (m + 1) * P, tokens], result[:])
+            for m, bank in enumerate(banks):
+                on_vector = m == 0 or g < VECTOR_GROUPS
+                result = keep.tile([P, tokens.stop - tokens.start], F32, name=f"result{g}_{m}")
+                copy = nc.vector.tensor_copy if on_vector else nc.scalar.copy
+                copy(result[:], bank[:])
+                queue = nc.sync if on_vector else nc.scalar
+                queue.dma_start(out[m * P : (m + 1) * P, tokens], result[:])
 
-        def first_out():
-            tokens = groups[0]
-            bank = psum.tile([P, N // P, CHUNK], F32, name="out0", tag="bank")
-            for m in range(N // P):
-                pass_out(bank[:, m, :], w1_codes, w1_plane, m, x_codes, x_plane, tokens, True)
-                pass_out(bank[:, m, :], w3_codes, w3_plane, m, h_codes, h_plane, tokens, False)
-            return bank
-
-        def first_store(bank):
-            result = keep.tile([P, N // P, CHUNK], F32, name="result0")
-            nc.vector.tensor_copy(result[:], bank[:])
-            for m in range(N // P):
-                nc.sync.dma_start(out[m * P : (m + 1) * P, groups[0]], result[:, m, :])
-
-        vector, scalar = nc.vector.tensor_copy, nc.scalar.copy
-        make_h(0)
-        make_h(1)
-        make_h(2)
-        quantise_h(0)
-        make_h(3)
-        make_h(4)
-        make_h(5)
-        quantise_h(1)
-        bank0 = first_out()
-        make_h(6)
-        quantise_h(2)
-        first_store(bank0)
-        open_out(1)
-        close_out(1)
-        make_h(7)
-        store_out(1, 0, vector, nc.sync)
-        store_out(1, 1, vector, nc.sync)
-        open_out(2)
-        close_out(2)
-        quantise_h(3)
-        store_out(2, 0, vector, nc.sync)
-        store_out(2, 1, scalar, nc.sync)
-        open_out(3)
-        open_out(4)
-        quantise_h(4)
-        close_out(3)
-        store_out(3, 0, vector, nc.sync)
-        store_out(3, 1, scalar, nc.sync)
-        close_out(4)
-        store_out(4, 0, vector, nc.sync)
-        store_out(4, 1, scalar, nc.scalar)
+        for chunk in range(LEAD):
+            make_h(chunk)
+            if chunk in VECTOR_CHUNKS:
+                quantise_h(VECTOR_CHUNKS.index(chunk))
+        for g in range(len(groups)):
+            banks = multiply_out(g)
+            if LEAD + g < CHUNKS:
+                make_h(LEAD + g)
+            store_out(g, banks)
+            if len(VECTOR_CHUNKS) + g < len(groups):
+                quantise_h(len(VECTOR_CHUNKS) + g)

@@ -28,6 +28,7 @@ VECTOR_CHUNKS = (1, 3)
 LEAD = BANKS - N // P
 VECTOR_GROUPS = 2
 WARM_PASSES = 4
+WARM_ROWS = 32
 
 
 def tile_picked_lora_none_p_kernel(
@@ -88,10 +89,10 @@ def tile_picked_lora_none_p_kernel(
             out=w2_codes[:].bitcast(FP8X4), scales=w2_plane[:], in_=w2_dealt[:].rearrange("p t m j -> p (t m j)")
         )
 
-        warm = psum.tile([P, H], F32, name="warm", tag="bank")
+        warm = psum.tile([WARM_ROWS, H], F32, name="warm", tag="bank")
         for turn in range(WARM_PASSES):
             nc.tensor.matmul_mx(
-                out=warm[:], lhsT=w2_codes[:, :P].bitcast(FP8X4), lhsT_scale=w2_plane[:, :P],
+                out=warm[:], lhsT=w2_codes[:, :WARM_ROWS].bitcast(FP8X4), lhsT_scale=w2_plane[:, :WARM_ROWS],
                 rhs=w2_codes[:].bitcast(FP8X4), rhs_scale=w2_plane[:], start=True, stop=True,
             )
 

@@ -20,13 +20,11 @@ PACK = 4
 PER_COLUMN = 16
 SCALE_ROWS = 16
 LANDING = P - SCALE_ROWS
-HALF = S // 2
+GROUP = 256
 CHUNK = 128
 CHUNKS = S // CHUNK
-GROUP_EDGES = (0, 1, 3, 5, 7, 8)
-VECTOR_CHUNKS = (1, 3)
-LEAD = BANKS - N // P
-VECTOR_GROUPS = 2
+VECTOR_CHUNKS = (2, 5)
+VECTOR_DEAL = 56
 WARM_PASSES = 4
 WARM_ROWS = 32
 
@@ -50,8 +48,6 @@ def tile_picked_lora_none_p_kernel(
         nc.vector.memset(xs_all[:LANDING, :].bitcast(I32), 0)
 
         planes = keep.tile([P, S + 2 * N], U8, name="planes", align_bytes=64)
-        nc.scalar.dma_start(planes[LANDING:, S : S + N].bitcast(I32), w1_scales[0].bitcast(I32))
-        nc.scalar.dma_start(planes[LANDING:, S + N :].bitcast(I32), w3_scales[0].bitcast(I32))
         nc.vector.memset(planes[:LANDING, S:].bitcast(I32), 0)
         x_plane, w1_plane, w3_plane = planes[:, :S], planes[:, S : S + N], planes[:, S + N :]
 
@@ -62,6 +58,8 @@ def tile_picked_lora_none_p_kernel(
 
         w2_raw = keep.tile([P, PACK, H], F32, name="w2_raw", align_bytes=64)
         nc.sync.dma_start(w2_raw[:], w2.rearrange("(p j) c -> p j c", j=PACK))
+        nc.sync.dma_start(planes[LANDING:, S : S + N].bitcast(I32), w1_scales[0].bitcast(I32))
+        nc.sync.dma_start(planes[LANDING:, S + N :].bitcast(I32), w3_scales[0].bitcast(I32))
         xw_all = keep.tile([P, T], I32, name="xw_all", align_bytes=64)
         nc.sync.dma_start(xw_all[:], words_of(x_words))
         w1_codes = keep.tile([P, N], I32, name="w1_codes", align_bytes=64)
@@ -80,9 +78,10 @@ def tile_picked_lora_none_p_kernel(
             )
 
         w2_dealt = keep.tile([P, PACK, P, PACK], BF16, name="w2_dealt", align_bytes=64)
-        nc.vector.tensor_copy(
-            w2_dealt[:].rearrange("p t m j -> p m t j"), w2_raw[:].rearrange("p j (m t) -> p m t j", t=PACK)
-        )
+        dealt = w2_dealt[:].rearrange("p t m j -> p m t j")
+        raw = w2_raw[:].rearrange("p j (m t) -> p m t j", t=PACK)
+        nc.vector.tensor_copy(dealt[:, :VECTOR_DEAL], raw[:, :VECTOR_DEAL])
+        nc.scalar.copy(dealt[:, VECTOR_DEAL:], raw[:, VECTOR_DEAL:])
         w2_codes = keep.tile([P, H], U32, name="w2_codes", align_bytes=64)
         w2_plane = keep.tile([P, H], U8, name="w2_plane", align_bytes=64)
         nc.vector.quantize_mx(
@@ -97,13 +96,12 @@ def tile_picked_lora_none_p_kernel(
             )
 
         x_codes = keep.tile([P, S], U32, name="x_codes", align_bytes=64)
-        for first in range(0, S, HALF):
+        for first in range(0, S, GROUP):
             nc.vector.tensor_copy(
-                x_codes[:, first : first + HALF],
-                xw_all[:].bitcast(U32).indirect(offsets[:, first // PER_COLUMN : (first + HALF) // PER_COLUMN]),
+                x_codes[:, first : first + GROUP],
+                xw_all[:].bitcast(U32).indirect(offsets[:, first // PER_COLUMN : (first + GROUP) // PER_COLUMN]),
             )
 
-        groups = [slice(a * CHUNK, b * CHUNK) for a, b in zip(GROUP_EDGES, GROUP_EDGES[1:])]
         h_rounded = keep.tile([P, S * PACK], BF16, name="h_rounded", align_bytes=64)
         h_codes = keep.tile([P, S], U32, name="h_codes", align_bytes=64)
         h_plane = keep.tile([P, S], U8, name="h_plane", align_bytes=64)
@@ -121,17 +119,15 @@ def tile_picked_lora_none_p_kernel(
             interleaved = h_rounded[:, tokens.start * PACK : tokens.stop * PACK].rearrange("p (n t) -> p n t", t=PACK)
             copy(interleaved, bank[:].rearrange("p t n -> p n t"))
 
-        def quantise_h(g):
-            tokens = groups[g]
+        def quantise_h(tokens):
             nc.vector.quantize_mx(
                 out=h_codes[:, tokens].bitcast(FP8X4), scales=h_plane[:, tokens],
                 in_=h_rounded[:, tokens.start * PACK : tokens.stop * PACK],
             )
 
-        def multiply_out(g):
-            tokens = groups[g]
+        def multiply_out(tokens):
             width = tokens.stop - tokens.start
-            banks = [psum.tile([P, width], F32, name=f"out{g}_{m}", tag="bank") for m in range(N // P)]
+            banks = [psum.tile([P, width], F32, name=f"out{tokens.start}_{m}", tag="bank") for m in range(N // P)]
             terms = ((w1_codes, w1_plane, x_codes, x_plane), (w3_codes, w3_plane, h_codes, h_plane))
             for term, (w_codes, w_plane, codes, plane) in enumerate(terms):
                 for m, bank in enumerate(banks):
@@ -143,24 +139,28 @@ def tile_picked_lora_none_p_kernel(
                     )
             return banks
 
-        def store_out(g, banks):
-            tokens = groups[g]
-            for m, bank in enumerate(banks):
-                on_vector = m == 0 or g < VECTOR_GROUPS
-                result = keep.tile([P, tokens.stop - tokens.start], F32, name=f"result{g}_{m}")
-                copy = nc.vector.tensor_copy if on_vector else nc.scalar.copy
-                copy(result[:], bank[:])
-                queue = nc.sync if on_vector else nc.scalar
-                queue.dma_start(out[m * P : (m + 1) * P, tokens], result[:])
+        def store_out(tokens, m, bank, copy, queue):
+            result = keep.tile([P, tokens.stop - tokens.start], F32, name=f"result{tokens.start}_{m}")
+            copy(result[:], bank[:])
+            queue.dma_start(out[m * P : (m + 1) * P, tokens], result[:])
 
-        for chunk in range(LEAD):
+        groups = [slice(first, first + GROUP) for first in range(0, S, GROUP)]
+        vector, scalar = nc.vector.tensor_copy, nc.scalar.copy
+        for chunk in range(4):
             make_h(chunk)
-            if chunk in VECTOR_CHUNKS:
-                quantise_h(VECTOR_CHUNKS.index(chunk))
-        for g in range(len(groups)):
-            banks = multiply_out(g)
-            if LEAD + g < CHUNKS:
-                make_h(LEAD + g)
-            store_out(g, banks)
-            if len(VECTOR_CHUNKS) + g < len(groups):
-                quantise_h(len(VECTOR_CHUNKS) + g)
+        quantise_h(groups[0])
+        quantise_h(groups[1])
+        for chunk in range(4, CHUNKS):
+            make_h(chunk)
+        banks0 = multiply_out(groups[0])
+        banks1 = multiply_out(groups[1])
+        store_out(groups[0], 0, banks0[0], vector, nc.sync)
+        quantise_h(groups[2])
+        store_out(groups[0], 1, banks0[1], vector, nc.sync)
+        quantise_h(groups[3])
+        store_out(groups[1], 0, banks1[0], scalar, nc.sync)
+        store_out(groups[1], 1, banks1[1], scalar, nc.scalar)
+        for g in (2, 3):
+            banks = multiply_out(groups[g])
+            store_out(groups[g], 0, banks[0], vector, nc.sync)
+            store_out(groups[g], 1, banks[1], scalar, nc.scalar)

@@ -24,7 +24,7 @@ GROUP = 256
 CHUNK = 128
 CHUNKS = S // CHUNK
 VECTOR_CHUNKS = (2, 5)
-VECTOR_DEAL = 56
+VECTOR_DEAL = 72
 WARM_PASSES = 4
 WARM_ROWS = 32
 
@@ -41,25 +41,24 @@ def tile_picked_lora_none_p_kernel(
             return dram[0].rearrange("p n t -> p (n t)").bitcast(I32)
 
         offsets = keep.tile([P, S // PER_COLUMN], U16, name="offsets")
-        nc.sync.dma_start(offsets[:], offs)
 
         xs_all = keep.tile([P, T], U8, name="xs_all", align_bytes=64)
         nc.sync.dma_start(xs_all[LANDING:, :].bitcast(I32), x_scales[0].bitcast(I32))
+        nc.sync.dma_start(offsets[:], offs)
         nc.vector.memset(xs_all[:LANDING, :].bitcast(I32), 0)
 
-        planes = keep.tile([P, S + 2 * N], U8, name="planes", align_bytes=64)
-        nc.vector.memset(planes[:LANDING, S:].bitcast(I32), 0)
-        x_plane, w1_plane, w3_plane = planes[:, :S], planes[:, S : S + N], planes[:, S + N :]
+        ws_all = keep.tile([P, 2 * N], U8, name="ws_all", align_bytes=64)
+        nc.scalar.dma_start(ws_all[LANDING:, :N].bitcast(I32), w1_scales[0].bitcast(I32))
+        nc.scalar.dma_start(ws_all[LANDING:, N:].bitcast(I32), w3_scales[0].bitcast(I32))
+        nc.vector.memset(ws_all[:LANDING, :].bitcast(I32), 0)
 
         seed = keep.tile([P, 2], F32, name="seed")
         nc.gpsimd.memset(seed[:], 0.0)
         primed = keep.tile([P, 2], BF16, name="primed")
         nc.scalar.copy(primed[:], seed[:])
 
-        w2_raw = keep.tile([P, PACK, H], F32, name="w2_raw", align_bytes=64)
+        w2_raw = keep.tile([P, PACK, H], F32, name="w2_raw", tag="reused", align_bytes=64)
         nc.sync.dma_start(w2_raw[:], w2.rearrange("(p j) c -> p j c", j=PACK))
-        nc.sync.dma_start(planes[LANDING:, S : S + N].bitcast(I32), w1_scales[0].bitcast(I32))
-        nc.sync.dma_start(planes[LANDING:, S + N :].bitcast(I32), w3_scales[0].bitcast(I32))
         xw_all = keep.tile([P, T], I32, name="xw_all", align_bytes=64)
         nc.sync.dma_start(xw_all[:], words_of(x_words))
         w1_codes = keep.tile([P, N], I32, name="w1_codes", align_bytes=64)
@@ -69,7 +68,17 @@ def tile_picked_lora_none_p_kernel(
 
         xs_picked = keep.tile([P, S], U8, name="xs_picked", align_bytes=64)
         nc.vector.tensor_copy(xs_picked[:], xs_all[:].indirect(offsets[:]))
+
+        w2_dealt = keep.tile([P, PACK, P, PACK], BF16, name="w2_dealt", align_bytes=64)
+        dealt = w2_dealt[:].rearrange("p t m j -> p m t j")
+        raw = w2_raw[:].rearrange("p j (m t) -> p m t j", t=PACK)
+        nc.vector.tensor_copy(dealt[:, :VECTOR_DEAL], raw[:, :VECTOR_DEAL])
+        nc.scalar.copy(dealt[:, VECTOR_DEAL:], raw[:, VECTOR_DEAL:])
+
+        planes = keep.tile([P, S + 2 * N], U8, name="planes", tag="reused", align_bytes=64)
+        x_plane, w1_plane, w3_plane = planes[:, :S], planes[:, S : S + N], planes[:, S + N :]
         nc.vector.tensor_copy(x_plane.bitcast(I32), xs_picked[:].bitcast(I32))
+        nc.vector.tensor_copy(planes[:, S:].bitcast(I32), ws_all[:].bitcast(I32))
         rows = SCALE_ROWS * QUADRANT // P
         for q in range(P // QUADRANT):
             nc.scalar.dma_start(
@@ -77,11 +86,6 @@ def tile_picked_lora_none_p_kernel(
                 planes[LANDING + rows * q : LANDING + rows * (q + 1), :].bitcast(I32),
             )
 
-        w2_dealt = keep.tile([P, PACK, P, PACK], BF16, name="w2_dealt", align_bytes=64)
-        dealt = w2_dealt[:].rearrange("p t m j -> p m t j")
-        raw = w2_raw[:].rearrange("p j (m t) -> p m t j", t=PACK)
-        nc.vector.tensor_copy(dealt[:, :VECTOR_DEAL], raw[:, :VECTOR_DEAL])
-        nc.scalar.copy(dealt[:, VECTOR_DEAL:], raw[:, VECTOR_DEAL:])
         w2_codes = keep.tile([P, H], U32, name="w2_codes", align_bytes=64)
         w2_plane = keep.tile([P, H], U8, name="w2_plane", align_bytes=64)
         nc.vector.quantize_mx(

@@ -16,16 +16,19 @@ FP8X4 = mybir.dt.float8_e4m3fn_x4
 P = 128
 BANKS = 8
 QUADRANT = 32
+QUADRANTS = P // QUADRANT
+ALIGN = 256
 PACK = 4
 PER_COLUMN = 16
 SCALE_ROWS = 16
+ROWS = SCALE_ROWS // QUADRANTS
 LANDING = P - SCALE_ROWS
 GROUP = 256
 CHUNK = 128
 CHUNKS = S // CHUNK
 VECTOR_CHUNKS = (2, 5)
 VECTOR_DEAL = 72
-WARM_PASSES = 4
+WARM_PASSES = 5
 WARM_ROWS = 32
 
 
@@ -42,55 +45,62 @@ def tile_picked_lora_none_p_kernel(
 
         offsets = keep.tile([P, S // PER_COLUMN], U16, name="offsets")
 
-        xs_all = keep.tile([P, T], U8, name="xs_all", align_bytes=64)
+        xs_all = keep.tile([P, T], U8, name="xs_all", align_bytes=ALIGN)
         nc.sync.dma_start(xs_all[LANDING:, :].bitcast(I32), x_scales[0].bitcast(I32))
         nc.sync.dma_start(offsets[:], offs)
-        nc.vector.memset(xs_all[:LANDING, :].bitcast(I32), 0)
 
-        ws_all = keep.tile([P, 2 * N], U8, name="ws_all", align_bytes=64)
-        nc.scalar.dma_start(ws_all[LANDING:, :N].bitcast(I32), w1_scales[0].bitcast(I32))
-        nc.scalar.dma_start(ws_all[LANDING:, N:].bitcast(I32), w3_scales[0].bitcast(I32))
-        nc.vector.memset(ws_all[:LANDING, :].bitcast(I32), 0)
+        ws_rows = keep.tile([ROWS, QUADRANTS, 2 * N], U8, name="ws_rows", align_bytes=ALIGN)
+        for side, scales in enumerate((w1_scales, w3_scales)):
+            nc.scalar.dma_start(
+                ws_rows[:, :, side * N : (side + 1) * N].bitcast(I32),
+                scales[0].bitcast(I32).rearrange("(q r) n -> r q n", r=ROWS),
+            )
+        nc.vector.memset(xs_all[:LANDING, :].bitcast(I32), 0)
 
         seed = keep.tile([P, 2], F32, name="seed")
         nc.gpsimd.memset(seed[:], 0.0)
         primed = keep.tile([P, 2], BF16, name="primed")
         nc.scalar.copy(primed[:], seed[:])
 
-        w2_raw = keep.tile([P, PACK, H], F32, name="w2_raw", tag="reused", align_bytes=64)
+        w2_raw = keep.tile([P, PACK, H], F32, name="w2_raw", tag="w2_bytes", align_bytes=ALIGN)
         nc.sync.dma_start(w2_raw[:], w2.rearrange("(p j) c -> p j c", j=PACK))
-        xw_all = keep.tile([P, T], I32, name="xw_all", align_bytes=64)
+        xw_all = keep.tile([P, T], I32, name="xw_all", align_bytes=ALIGN)
         nc.sync.dma_start(xw_all[:], words_of(x_words))
-        w1_codes = keep.tile([P, N], I32, name="w1_codes", align_bytes=64)
+        w1_codes = keep.tile([P, N], I32, name="w1_codes", align_bytes=ALIGN)
         nc.sync.dma_start(w1_codes[:], words_of(w1_words))
-        w3_codes = keep.tile([P, N], I32, name="w3_codes", align_bytes=64)
+        w3_codes = keep.tile([P, N], I32, name="w3_codes", align_bytes=ALIGN)
         nc.sync.dma_start(w3_codes[:], words_of(w3_words))
 
-        xs_picked = keep.tile([P, S], U8, name="xs_picked", align_bytes=64)
+        xs_picked = keep.tile([P, S], U8, name="xs_picked", align_bytes=ALIGN)
         nc.vector.tensor_copy(xs_picked[:], xs_all[:].indirect(offsets[:]))
 
-        w2_dealt = keep.tile([P, PACK, P, PACK], BF16, name="w2_dealt", align_bytes=64)
+        w2_dealt = keep.tile([P, PACK, P, PACK], BF16, name="w2_dealt", tag="reused", align_bytes=ALIGN)
         dealt = w2_dealt[:].rearrange("p t m j -> p m t j")
         raw = w2_raw[:].rearrange("p j (m t) -> p m t j", t=PACK)
         nc.vector.tensor_copy(dealt[:, :VECTOR_DEAL], raw[:, :VECTOR_DEAL])
         nc.scalar.copy(dealt[:, VECTOR_DEAL:], raw[:, VECTOR_DEAL:])
 
-        planes = keep.tile([P, S + 2 * N], U8, name="planes", tag="reused", align_bytes=64)
-        x_plane, w1_plane, w3_plane = planes[:, :S], planes[:, S : S + N], planes[:, S + N :]
-        nc.vector.tensor_copy(x_plane.bitcast(I32), xs_picked[:].bitcast(I32))
-        nc.vector.tensor_copy(planes[:, S:].bitcast(I32), ws_all[:].bitcast(I32))
-        rows = SCALE_ROWS * QUADRANT // P
-        for q in range(P // QUADRANT):
+        x_plane = keep.tile([P, S], U8, name="x_plane", tag="w2_bytes", align_bytes=ALIGN)
+        nc.vector.memset(x_plane[:].bitcast(I32), 0)
+        for q in range(QUADRANTS):
             nc.scalar.dma_start(
-                planes[QUADRANT * q : QUADRANT * q + rows, :].bitcast(I32),
-                planes[LANDING + rows * q : LANDING + rows * (q + 1), :].bitcast(I32),
+                x_plane[QUADRANT * q : QUADRANT * q + ROWS, :].bitcast(I32),
+                xs_picked[LANDING + ROWS * q : LANDING + ROWS * (q + 1), :].bitcast(I32),
             )
 
-        w2_codes = keep.tile([P, H], U32, name="w2_codes", align_bytes=64)
-        w2_plane = keep.tile([P, H], U8, name="w2_plane", align_bytes=64)
+        w2_codes = keep.tile([P, H], U32, name="w2_codes", align_bytes=ALIGN)
+        w2_plane = keep.tile([P, H], U8, name="w2_plane", align_bytes=ALIGN)
         nc.vector.quantize_mx(
             out=w2_codes[:].bitcast(FP8X4), scales=w2_plane[:], in_=w2_dealt[:].rearrange("p t m j -> p (t m j)")
         )
+
+        w_planes = keep.tile([P, 2 * N], U8, name="w_planes", tag="reused", align_bytes=ALIGN)
+        w1_plane, w3_plane = w_planes[:, :N], w_planes[:, N:]
+        nc.vector.memset(w_planes[:].bitcast(I32), 0)
+        for q in range(QUADRANTS):
+            nc.vector.tensor_copy(
+                w_planes[QUADRANT * q : QUADRANT * q + ROWS, :].bitcast(I32), ws_rows[:, q, :].bitcast(I32)
+            )
 
         warm = psum.tile([WARM_ROWS, H], F32, name="warm", tag="bank")
         for turn in range(WARM_PASSES):
@@ -99,16 +109,16 @@ def tile_picked_lora_none_p_kernel(
                 rhs=w2_codes[:].bitcast(FP8X4), rhs_scale=w2_plane[:], start=True, stop=True,
             )
 
-        x_codes = keep.tile([P, S], U32, name="x_codes", align_bytes=64)
+        x_codes = keep.tile([P, S], U32, name="x_codes", align_bytes=ALIGN)
         for first in range(0, S, GROUP):
             nc.vector.tensor_copy(
                 x_codes[:, first : first + GROUP],
                 xw_all[:].bitcast(U32).indirect(offsets[:, first // PER_COLUMN : (first + GROUP) // PER_COLUMN]),
             )
 
-        h_rounded = keep.tile([P, S * PACK], BF16, name="h_rounded", align_bytes=64)
-        h_codes = keep.tile([P, S], U32, name="h_codes", align_bytes=64)
-        h_plane = keep.tile([P, S], U8, name="h_plane", align_bytes=64)
+        h_rounded = keep.tile([P, S * PACK], BF16, name="h_rounded", align_bytes=ALIGN)
+        h_codes = keep.tile([P, S], U32, name="h_codes", align_bytes=ALIGN)
+        h_plane = keep.tile([P, S], U8, name="h_plane", align_bytes=ALIGN)
 
         def make_h(chunk):
             bank = psum.tile([P, PACK, CHUNK], F32, name=f"h{chunk}", tag="bank")
@@ -144,7 +154,7 @@ def tile_picked_lora_none_p_kernel(
             return banks
 
         def store_out(tokens, m, bank, copy, queue):
-            result = keep.tile([P, tokens.stop - tokens.start], F32, name=f"result{tokens.start}_{m}")
+            result = keep.tile([P, tokens.stop - tokens.start], F32, name=f"result{tokens.start}_{m}", align_bytes=ALIGN)
             copy(result[:], bank[:])
             queue.dma_start(out[m * P : (m + 1) * P, tokens], result[:])
 

@@ -80,6 +80,12 @@ def tile_picked_lora_none_p_kernel(
         nc.vector.tensor_copy(dealt[:, :VECTOR_DEAL], raw[:, :VECTOR_DEAL])
         nc.scalar.copy(dealt[:, VECTOR_DEAL:], raw[:, VECTOR_DEAL:])
 
+        w2_codes = keep.tile([P, H], U32, name="w2_codes", align_bytes=ALIGN)
+        w2_plane = keep.tile([P, H], U8, name="w2_plane", align_bytes=ALIGN)
+        nc.vector.quantize_mx(
+            out=w2_codes[:].bitcast(FP8X4), scales=w2_plane[:], in_=w2_dealt[:].rearrange("p t m j -> p (t m j)")
+        )
+
         x_plane = keep.tile([P, S], U8, name="x_plane", tag="w2_bytes", align_bytes=ALIGN)
         nc.vector.memset(x_plane[:].bitcast(I32), 0)
         for q in range(QUADRANTS):
@@ -87,12 +93,6 @@ def tile_picked_lora_none_p_kernel(
                 x_plane[QUADRANT * q : QUADRANT * q + ROWS, :].bitcast(I32),
                 xs_picked[LANDING + ROWS * q : LANDING + ROWS * (q + 1), :].bitcast(I32),
             )
-
-        w2_codes = keep.tile([P, H], U32, name="w2_codes", align_bytes=ALIGN)
-        w2_plane = keep.tile([P, H], U8, name="w2_plane", align_bytes=ALIGN)
-        nc.vector.quantize_mx(
-            out=w2_codes[:].bitcast(FP8X4), scales=w2_plane[:], in_=w2_dealt[:].rearrange("p t m j -> p (t m j)")
-        )
 
         w_planes = keep.tile([P, 2 * N], U8, name="w_planes", tag="reused", align_bytes=ALIGN)
         w1_plane, w3_plane = w_planes[:, :N], w_planes[:, N:]

from contextlib import ExitStack

import concourse.mybir as mybir

K, T, S, H, N = 512, 4096, 1024, 512, 256
FLOPS = 2 * S * (K * H + K * N + H * N)

F32 = mybir.dt.float32
BF16 = mybir.dt.bfloat16
I32 = mybir.dt.int32
U32 = mybir.dt.uint32
U16 = mybir.dt.uint16
U8 = mybir.dt.uint8
FP8X4 = mybir.dt.float8_e4m3fn_x4

P = 128
BANKS = 8
QUADRANT = 32
QUADRANTS = P // QUADRANT
ALIGN = 256
PACK = 4
PER_COLUMN = 16
SCALE_ROWS = 16
ROWS = SCALE_ROWS // QUADRANTS
LANDING = P - SCALE_ROWS
GROUP = 256
CHUNK = 128
CHUNKS = S // CHUNK
VECTOR_CHUNKS = (2, 5)
VECTOR_DEAL = 72
WARM_PASSES = 5
WARM_ROWS = 32


def tile_picked_lora_none_p_kernel(
    tc, x_words, x_scales, w1_words, w1_scales, w2, w3_words, w3_scales, offs, out
):
    nc = tc.nc
    with ExitStack() as ctx:
        keep = ctx.enter_context(tc.tile_pool(name="keep", bufs=1))
        psum = ctx.enter_context(tc.psum_pool(name="psum", bufs=BANKS))

        def words_of(dram):
            return dram[0].rearrange("p n t -> p (n t)").bitcast(I32)

        offsets = keep.tile([P, S // PER_COLUMN], U16, name="offsets")

        xs_all = keep.tile([P, T], U8, name="xs_all", align_bytes=ALIGN)
        nc.sync.dma_start(xs_all[LANDING:, :].bitcast(I32), x_scales[0].bitcast(I32))
        nc.sync.dma_start(offsets[:], offs)

        ws_rows = keep.tile([ROWS, QUADRANTS, 2 * N], U8, name="ws_rows", align_bytes=ALIGN)
        for side, scales in enumerate((w1_scales, w3_scales)):
            nc.scalar.dma_start(
                ws_rows[:, :, side * N : (side + 1) * N].bitcast(I32),
                scales[0].bitcast(I32).rearrange("(q r) n -> r q n", r=ROWS),
            )
        nc.vector.memset(xs_all[:LANDING, :].bitcast(I32), 0)

        seed = keep.tile([P, 2], F32, name="seed")
        nc.gpsimd.memset(seed[:], 0.0)
        primed = keep.tile([P, 2], BF16, name="primed")
        nc.scalar.copy(primed[:], seed[:])

        w2_raw = keep.tile([P, PACK, H], F32, name="w2_raw", tag="w2_bytes", align_bytes=ALIGN)
        nc.sync.dma_start(w2_raw[:], w2.rearrange("(p j) c -> p j c", j=PACK))
        xw_all = keep.tile([P, T], I32, name="xw_all", align_bytes=ALIGN)
        nc.sync.dma_start(xw_all[:], words_of(x_words))
        w1_codes = keep.tile([P, N], I32, name="w1_codes", align_bytes=ALIGN)
        nc.sync.dma_start(w1_codes[:], words_of(w1_words))
        w3_codes = keep.tile([P, N], I32, name="w3_codes", align_bytes=ALIGN)
        nc.sync.dma_start(w3_codes[:], words_of(w3_words))

        xs_picked = keep.tile([P, S], U8, name="xs_picked", align_bytes=ALIGN)
        nc.vector.tensor_copy(xs_picked[:], xs_all[:].indirect(offsets[:]))

        w2_dealt = keep.tile([P, PACK, P, PACK], BF16, name="w2_dealt", tag="reused", align_bytes=ALIGN)
        dealt = w2_dealt[:].rearrange("p t m j -> p m t j")
        raw = w2_raw[:].rearrange("p j (m t) -> p m t j", t=PACK)
        nc.vector.tensor_copy(dealt[:, :VECTOR_DEAL], raw[:, :VECTOR_DEAL])
        nc.scalar.copy(dealt[:, VECTOR_DEAL:], raw[:, VECTOR_DEAL:])

        w2_codes = keep.tile([P, H], U32, name="w2_codes", align_bytes=ALIGN)
        w2_plane = keep.tile([P, H], U8, name="w2_plane", align_bytes=ALIGN)
        nc.vector.quantize_mx(
            out=w2_codes[:].bitcast(FP8X4), scales=w2_plane[:], in_=w2_dealt[:].rearrange("p t m j -> p (t m j)")
        )

        x_plane = keep.tile([P, S], U8, name="x_plane", tag="w2_bytes", align_bytes=ALIGN)
        nc.vector.memset(x_plane[:].bitcast(I32), 0)
        for q in range(QUADRANTS):
            nc.scalar.dma_start(
                x_plane[QUADRANT * q : QUADRANT * q + ROWS, :].bitcast(I32),
                xs_picked[LANDING + ROWS * q : LANDING + ROWS * (q + 1), :].bitcast(I32),
            )

        w_planes = keep.tile([P, 2 * N], U8, name="w_planes", tag="reused", align_bytes=ALIGN)
        w1_plane, w3_plane = w_planes[:, :N], w_planes[:, N:]
        nc.vector.memset(w_planes[:].bitcast(I32), 0)
        for q in range(QUADRANTS):
            nc.vector.tensor_copy(
                w_planes[QUADRANT * q : QUADRANT * q + ROWS, :].bitcast(I32), ws_rows[:, q, :].bitcast(I32)
            )

        warm = psum.tile([WARM_ROWS, H], F32, name="warm", tag="bank")
        for turn in range(WARM_PASSES):
            nc.tensor.matmul_mx(
                out=warm[:], lhsT=w2_codes[:, :WARM_ROWS].bitcast(FP8X4), lhsT_scale=w2_plane[:, :WARM_ROWS],
                rhs=w2_codes[:].bitcast(FP8X4), rhs_scale=w2_plane[:], start=True, stop=True,
            )

        x_codes = keep.tile([P, S], U32, name="x_codes", align_bytes=ALIGN)
        for first in range(0, S, GROUP):
            nc.vector.tensor_copy(
                x_codes[:, first : first + GROUP],
                xw_all[:].bitcast(U32).indirect(offsets[:, first // PER_COLUMN : (first + GROUP) // PER_COLUMN]),
            )

        h_rounded = keep.tile([P, S * PACK], BF16, name="h_rounded", align_bytes=ALIGN)
        h_codes = keep.tile([P, S], U32, name="h_codes", align_bytes=ALIGN)
        h_plane = keep.tile([P, S], U8, name="h_plane", align_bytes=ALIGN)

        def make_h(chunk):
            bank = psum.tile([P, PACK, CHUNK], F32, name=f"h{chunk}", tag="bank")
            tokens = slice(chunk * CHUNK, (chunk + 1) * CHUNK)
            for t in range(PACK):
                cols = slice(t * P, (t + 1) * P)
                nc.tensor.matmul_mx(
                    out=bank[:, t, :], lhsT=w2_codes[:, cols].bitcast(FP8X4), lhsT_scale=w2_plane[:, cols],
                    rhs=x_codes[:, tokens].bitcast(FP8X4), rhs_scale=x_plane[:, tokens], start=True, stop=True,
                )
            copy = nc.vector.tensor_copy if chunk in VECTOR_CHUNKS else nc.scalar.copy
            interleaved = h_rounded[:, tokens.start * PACK : tokens.stop * PACK].rearrange("p (n t) -> p n t", t=PACK)
            copy(interleaved, bank[:].rearrange("p t n -> p n t"))

        def quantise_h(tokens):
            nc.vector.quantize_mx(
                out=h_codes[:, tokens].bitcast(FP8X4), scales=h_plane[:, tokens],
                in_=h_rounded[:, tokens.start * PACK : tokens.stop * PACK],
            )

        def multiply_out(tokens):
            width = tokens.stop - tokens.start
            banks = [psum.tile([P, width], F32, name=f"out{tokens.start}_{m}", tag="bank") for m in range(N // P)]
            terms = ((w1_codes, w1_plane, x_codes, x_plane), (w3_codes, w3_plane, h_codes, h_plane))
            for term, (w_codes, w_plane, codes, plane) in enumerate(terms):
                for m, bank in enumerate(banks):
                    cols = slice(m * P, (m + 1) * P)
                    nc.tensor.matmul_mx(
                        out=bank[:], lhsT=w_codes[:, cols].bitcast(FP8X4), lhsT_scale=w_plane[:, cols],
                        rhs=codes[:, tokens].bitcast(FP8X4), rhs_scale=plane[:, tokens],
                        start=term == 0, stop=term == len(terms) - 1,
                    )
            return banks

        def store_out(tokens, m, bank, copy, queue):
            result = keep.tile([P, tokens.stop - tokens.start], F32, name=f"result{tokens.start}_{m}", align_bytes=ALIGN)
            copy(result[:], bank[:])
            queue.dma_start(out[m * P : (m + 1) * P, tokens], result[:])

        groups = [slice(first, first + GROUP) for first in range(0, S, GROUP)]
        vector, scalar = nc.vector.tensor_copy, nc.scalar.copy
        for chunk in range(4):
            make_h(chunk)
        quantise_h(groups[0])
        quantise_h(groups[1])
        for chunk in range(4, CHUNKS):
            make_h(chunk)
        banks0 = multiply_out(groups[0])
        banks1 = multiply_out(groups[1])
        store_out(groups[0], 0, banks0[0], vector, nc.sync)
        quantise_h(groups[2])
        store_out(groups[0], 1, banks0[1], vector, nc.sync)
        quantise_h(groups[3])
        store_out(groups[1], 0, banks1[0], scalar, nc.sync)
        store_out(groups[1], 1, banks1[1], scalar, nc.scalar)
        for g in (2, 3):
            banks = multiply_out(groups[g])
            store_out(groups[g], 0, banks[0], vector, nc.sync)
            store_out(groups[g], 1, banks[1], scalar, nc.scalar)
